import numpy as np
import ml_dtypes


def mxq(x, axis, fmt="e4m3"):
    dtype, down = {"e4m3": (ml_dtypes.float8_e4m3fn, 7), "e5m2": (ml_dtypes.float8_e5m2, 14)}[fmt]
    v = np.moveaxis(np.asarray(x, np.float32).astype(ml_dtypes.bfloat16).astype(np.float64), axis, -1)
    blocks = v.reshape(v.shape[:-1] + (-1, 32))
    amax = np.abs(blocks).max(-1, keepdims=True)
    byte = np.maximum(np.where(amax > 0, np.frexp(amax)[1] - 1 + 127, 0) - down, 1)
    scale = np.exp2(byte - 127.0)
    codes = (blocks / scale).astype(np.float32).astype(dtype).astype(np.float64)
    return np.moveaxis((codes * scale).reshape(v.shape), -1, axis)


WIDE = False


def mx_kscale(k):
    if not WIDE:
        return np.ones(k)
    levels = np.array([10, -10, 5, -5, 0])
    if k % 512:
        return np.exp2(np.random.permutation(np.resize(levels, k // 32))).repeat(32)
    a = np.empty((k // 512, 16))
    for p in range(k // 512):
        a[p, :8] = np.random.permutation(np.resize(levels, 8))
        for g in range(8):
            far = levels[np.abs(levels - a[p, g]) >= 10]
            a[p, g + 8] = far[np.random.randint(len(far))]
    return np.exp2(a.ravel()).repeat(32)


def f64(x):
    return np.asarray(x).astype(np.float64)


def striped(idx):
    return np.tile(idx.reshape(-1, 16).T, (8, 1)).astype(np.uint16)


def unstriped(offs):
    return offs[:16].T.reshape(-1).astype(np.int64)


def pack_weight(w):
    k, n = w.shape
    w = f64(np.asarray(w, np.float32).astype(ml_dtypes.bfloat16)).reshape(k // 32, 32, n)
    amax = np.abs(w).max(1)
    byte = np.clip(np.where(amax > 0, np.frexp(amax)[1] - 1 + 127 - 7, 1), 1, 254)
    scaled = (w * np.exp2(127.0 - byte)[:, None, :]).reshape(k, n).astype(np.float32)
    words = np.ascontiguousarray(scaled.reshape(k // 512, 128, 4, n).transpose(0, 1, 3, 2)).astype(ml_dtypes.float8_e4m3fn).view(np.uint8)
    return words, np.ascontiguousarray(byte.astype(np.uint8).reshape(k // 512, 16, n))


def unpack_weight(words, scales):
    g, p, n, _ = words.shape
    vals = np.ascontiguousarray(words).view(ml_dtypes.float8_e4m3fn).astype(np.float64) * np.repeat(np.exp2(scales.astype(np.float64) - 127.0), 8, axis=1)[..., None]
    return vals.transpose(0, 1, 3, 2).reshape(g * 512, n)


def relu(v):
    return np.maximum(v, 0.0)


V, K, T, S, N = 512, 1024, 2048, 1024, 256


def setup_inputs():
    n = np.random.standard_normal
    s = mx_kscale(K)[:, None]
    near = np.random.permutation(S)
    packed_xT = pack_weight(n((K, T)) * s)
    return {
        "x_words": packed_xT[0],
        "x_scales": packed_xT[1],
        "w1": (n((K, N)) / np.sqrt(K) / s).astype(np.float32),
        "thr": (-np.random.uniform(0.2, 0.8, (N, 1))).astype(np.float32),
        "offs": striped(np.random.permutation(T)[:S]),
        "ev": striped(near[:V]),
        "od": striped(near[V:]),
    }


def reference(x_words, x_scales, w1, thr, offs, ev, od):
    xq = unpack_weight(x_words, x_scales)[:, unstriped(offs)]
    y = mxq(f64(w1), 0, "e4m3").T @ xq
    odd = y[:, unstriped(od)]
    evn = y[:, unstriped(ev)]
    det = odd - (0.5 * (evn + np.pad(evn, ((0, 0), (0, 1)))[:, 1:]))
    dth = relu(det + f64(thr)) - (relu(-1.0 * det + f64(thr)))
    smo = evn + 0.25 * (det + np.pad(det, ((0, 0), (1, 0)))[:, :V])
    ev2 = smo - (0.25 * (dth + np.pad(dth, ((0, 0), (1, 0)))[:, :V]))
    return dth + 0.5 * (ev2 + np.pad(ev2, ((0, 0), (0, 1)))[:, 1:])

@@ -1,0 +1,205 @@
+from contextlib import ExitStack
+
+import concourse.mybir as mybir
+
+K, T, S, N, V = 1024, 2048, 1024, 256, 512
+FLOPS = 2 * K * S * N
+
+F32 = mybir.dt.float32
+BF16 = mybir.dt.bfloat16
+I32 = mybir.dt.int32
+U32 = mybir.dt.uint32
+U16 = mybir.dt.uint16
+U8 = mybir.dt.uint8
+FP8X4 = mybir.dt.float8_e4m3fn_x4
+ALU = mybir.AluOpType
+ACT = mybir.ActivationFunctionType
+
+P = 128
+PASSES = 2
+BANDS = N // P
+PIECES = ((0, 512), (512, 768), (768, 1024))
+PAD = 8
+
+
+def tile_picked_ylift5_odd_p_kernel(tc, x_words, x_scales, w1, thr, offs, ev, od, out):
+    nc = tc.nc
+    with ExitStack() as ctx:
+        keep = ctx.enter_context(tc.tile_pool(name="keep", bufs=1))
+        psum = ctx.enter_context(tc.psum_pool(name="psum", bufs=1))
+
+        offs_t = keep.tile([P, S // 16], U16, name="offs_t")
+        ev_t = keep.tile([P, V // 16], U16, name="ev_t")
+        od_t = keep.tile([P, V // 16], U16, name="od_t")
+        xw = [keep.tile([P, T], I32, name="xw%d" % o, align_bytes=64) for o in range(PASSES)]
+        xs = keep.tile([P, T], U8, name="xs", align_bytes=64)
+        wraw = [keep.tile([P, 4, N], F32, name="wraw%d" % o, align_bytes=64) for o in range(PASSES)]
+        thr_t = keep.tile([P, BANDS], F32, name="thr_t")
+
+        nc.gpsimd.memset(xs[:, 0 : T // 2].bitcast(I32), 0)
+        nc.vector.memset(xs[:, T // 2 : T].bitcast(I32), 0)
+
+        def load_words(o):
+            nc.sync.dma_start(out=xw[o][:], in_=x_words[o].rearrange("p n t -> p (n t)").bitcast(I32))
+
+        def load_w(o):
+            nc.sync.dma_start(out=wraw[o][:], in_=w1[512 * o : 512 * (o + 1), :].rearrange("(p j) n -> p j n", j=4))
+
+        nc.sync.dma_start(offs_t[:], offs)
+        nc.sync.dma_start(ev_t[:], ev)
+        nc.sync.dma_start(od_t[:], od)
+        for q in range(4):
+            nc.sync.dma_start(
+                out=xs[32 * q : 32 * q + 8, :].bitcast(I32),
+                in_=x_scales[:, 4 * q : 4 * q + 4, :].bitcast(I32),
+            )
+        load_words(0)
+        load_w(0)
+        load_words(1)
+        load_w(1)
+        with nc.allow_non_contiguous_dma(reason="one threshold a partition"):
+            nc.gpsimd.dma_start(out=thr_t[:], in_=thr.rearrange("(b p) one -> p (b one)", p=P))
+
+        hi = keep.tile([P, BANDS], F32, name="hi")
+        lo = keep.tile([P, BANDS], F32, name="lo")
+        sg = keep.tile([P, BANDS], F32, name="sg")
+        gain = keep.tile([P, BANDS], F32, name="gain")
+        nc.scalar.activation(hi[:], thr_t[:], ACT.Abs)
+        nc.scalar.activation(lo[:], hi[:], ACT.Copy, scale=-1.0)
+        nc.scalar.activation(sg[:], thr_t[:], ACT.Sign)
+        nc.scalar.activation(gain[:], sg[:], ACT.Copy, scale=-0.125)
+
+        evn = [keep.tile([P, V + PAD], F32, name="evn%d" % b, align_bytes=64) for b in range(BANDS)]
+        odd = [keep.tile([P, V], F32, name="odd%d" % b, align_bytes=64) for b in range(BANDS)]
+        clip = [keep.tile([P, V + 2 * PAD], F32, name="clip%d" % b, align_bytes=64) for b in range(BANDS)]
+        for b in range(BANDS):
+            nc.gpsimd.memset(evn[b][:, V : V + PAD], 0.0)
+            nc.gpsimd.memset(clip[b][:, 0:PAD], 0.0)
+
+        wq = {}
+        ws = {}
+        wbf = {}
+
+        def round_w(o, m0, m1):
+            wbf[o, m0] = keep.tile([P, (m1 - m0) * 4], BF16, name="wbf%d_%d" % (o, m0), align_bytes=64)
+            nc.scalar.copy(
+                out=wbf[o, m0][:].rearrange("p (c i t) -> p c t i", i=4, t=4),
+                in_=wraw[o][:, :, m0:m1].rearrange("p t (c i) -> p c t i", i=4),
+            )
+
+        def quant_w(o, m0, m1):
+            codes = keep.tile([P, m1 - m0], U32, name="wq%d_%d" % (o, m0), align_bytes=64)
+            scales = keep.tile([P, m1 - m0], U8, name="ws%d_%d" % (o, m0), align_bytes=64)
+            nc.vector.quantize_mx(out=codes[:].bitcast(FP8X4), scales=scales[:], in_=wbf[o, m0][:])
+            for m in range(m0, m1, P):
+                wq[o, m // P] = codes[:, m - m0 : m - m0 + P]
+                ws[o, m // P] = scales[:, m - m0 : m - m0 + P]
+
+        gw = {}
+
+        def gather_words(o, a, b):
+            g = keep.tile([P, b - a], U32, name="gw%d_%d" % (o, a), align_bytes=64)
+            nc.vector.tensor_copy(g[:], xw[o][:].bitcast(U32).indirect(offs_t[:, a // 16 : b // 16]))
+            for lo_c, hi_c in PIECES:
+                if a <= lo_c and hi_c <= b:
+                    gw[o, lo_c] = g[:, lo_c - a : hi_c - a]
+
+        gs = keep.tile([P, S], U8, name="gs", align_bytes=64)
+        acc = {}
+        for b in range(BANDS):
+            for a, e in PIECES:
+                acc[b, a] = psum.tile([P, 512], F32, name="acc%d_%d" % (b, a))
+
+        def mm(o, b, a, e):
+            nc.tensor.matmul_mx(
+                out=acc[b, a][:, 0 : e - a],
+                lhsT=wq[o, b].bitcast(FP8X4),
+                lhsT_scale=ws[o, b],
+                rhs=gw[o, a].bitcast(FP8X4),
+                rhs_scale=gs[4 * o : P, a:e],
+                start=(o == 0),
+                stop=(o == PASSES - 1),
+            )
+
+        y = [keep.tile([P, S], F32, name="y%d" % b, align_bytes=64) for b in range(BANDS)]
+
+        nc.vector.tensor_copy(gs[:], xs[:].indirect(offs_t[:]))
+        gather_words(0, 0, S)
+        for o in range(PASSES):
+            for b in range(BANDS):
+                round_w(o, P * b, P * (b + 1))
+        quant_w(0, 0, P)
+        for a, e in PIECES:
+            mm(0, 0, a, e)
+        gather_words(1, 0, 512)
+        quant_w(1, 0, P)
+        gather_words(1, 512, 768)
+        gather_words(1, 768, 1024)
+        for a, e in PIECES:
+            mm(1, 0, a, e)
+            nc.scalar.copy(out=y[0][:, a:e], in_=acc[0, a][:, 0 : e - a])
+        quant_w(0, P, N)
+        quant_w(1, P, N)
+        for o in range(PASSES):
+            for a, e in PIECES:
+                mm(o, 1, a, e)
+                if o == PASSES - 1:
+                    nc.scalar.copy(out=y[1][:, a:e], in_=acc[1, a][:, 0 : e - a])
+
+        pair = [keep.tile([P, V], F32, name="pair%d" % b, align_bytes=64) for b in range(BANDS)]
+        det = [keep.tile([P, V], F32, name="det%d" % b, align_bytes=64) for b in range(BANDS)]
+        t1 = [keep.tile([P, V], F32, name="t1_%d" % b, align_bytes=64) for b in range(BANDS)]
+        t2 = [keep.tile([P, V], F32, name="t2_%d" % b, align_bytes=64) for b in range(BANDS)]
+        res = [keep.tile([P, V], F32, name="res%d" % b, align_bytes=64) for b in range(BANDS)]
+
+        def g_ev(b):
+            nc.vector.tensor_copy(evn[b][:, 0:V], y[b][:].indirect(ev_t[:]))
+
+        def g_od(b):
+            nc.vector.tensor_copy(odd[b][:], y[b][:].indirect(od_t[:]))
+
+        def s_pair(b):
+            nc.vector.tensor_tensor(pair[b][:], evn[b][:, 0:V], evn[b][:, 1 : V + 1], ALU.add)
+
+        def s_det(b):
+            nc.vector.scalar_tensor_tensor(det[b][:], pair[b][:], -0.5, odd[b][:], ALU.mult, ALU.add)
+
+        def s_clip(b):
+            nc.vector.tensor_scalar(
+                clip[b][:, PAD : PAD + V], det[b][:], lo[:, b : b + 1], hi[:, b : b + 1], ALU.max, ALU.min
+            )
+            nc.scalar.activation(
+                clip[b][:, PAD + V : PAD + V + 1], clip[b][:, PAD + V - 1 : PAD + V], ACT.Copy, scale=-1.0
+            )
+
+        def s_t1(b, a, e):
+            nc.vector.scalar_tensor_tensor(
+                t1[b][:, a:e], clip[b][:, PAD + a : PAD + e], -6.0, clip[b][:, PAD + a - 1 : PAD + e - 1], ALU.mult, ALU.add
+            )
+
+        def s_t2(b, a, e):
+            nc.vector.tensor_tensor(t2[b][:, a:e], t1[b][:, a:e], clip[b][:, PAD + a + 1 : PAD + e + 1], ALU.add)
+
+        def s_out(b, a, e):
+            nc.vector.scalar_tensor_tensor(
+                res[b][:, a:e], t2[b][:, a:e], gain[:, b : b + 1], odd[b][:, a:e], ALU.mult, ALU.add
+            )
+            nc.sync.dma_start(out=out[P * b : P * (b + 1), a:e], in_=res[b][:, a:e])
+
+        g_ev(0)
+        g_od(0)
+        s_pair(0)
+        g_ev(1)
+        s_det(0)
+        g_od(1)
+        s_clip(0)
+        s_pair(1)
+        s_t1(0, 0, V)
+        s_det(1)
+        s_t2(0, 0, V)
+        s_clip(1)
+        s_out(0, 0, V)
+        halves = ((0, V // 2), (V // 2, V))
+        for step in (s_t1, s_t2, s_out):
+            for a, e in halves:
+                step(1, a, e)

@@ -1,6 +1,7 @@
 from contextlib import ExitStack
 
 import concourse.mybir as mybir
+from concourse.masks import make_identity
 
 K, T, S, N, V = 1024, 2048, 1024, 256, 512
 FLOPS = 2 * K * S * N
@@ -19,6 +20,7 @@ P = 128
 PASSES = 2
 BANDS = N // P
 PIECES = ((0, 512), (512, 768), (768, 1024))
+GROUPS = (((0, 512), (512, 768), (768, 896), (896, 1024)), ((0, 512), (512, 1024)))
 PAD = 8
 
 
@@ -33,7 +35,7 @@ def tile_picked_ylift5_odd_p_kernel(tc, x_words, x_scales, w1, thr, offs, ev, od
         od_t = keep.tile([P, V // 16], U16, name="od_t")
         xw = [keep.tile([P, T], I32, name="xw%d" % o, align_bytes=64) for o in range(PASSES)]
         xs = keep.tile([P, T], U8, name="xs", align_bytes=64)
-        wraw = [keep.tile([P, 4, N], F32, name="wraw%d" % o, align_bytes=64) for o in range(PASSES)]
+        wraw = {}
         thr_t = keep.tile([P, BANDS], F32, name="thr_t")
 
         nc.gpsimd.memset(xs[:, 0 : T // 2].bitcast(I32), 0)
@@ -42,8 +44,10 @@ def tile_picked_ylift5_odd_p_kernel(tc, x_words, x_scales, w1, thr, offs, ev, od
         def load_words(o):
             nc.sync.dma_start(out=xw[o][:], in_=x_words[o].rearrange("p n t -> p (n t)").bitcast(I32))
 
-        def load_w(o):
-            nc.sync.dma_start(out=wraw[o][:], in_=w1[512 * o : 512 * (o + 1), :].rearrange("(p j) n -> p j n", j=4))
+        def load_w(o, b):
+            wraw[o, b] = keep.tile([P, 4, P], F32, name="wraw%d_%d" % (o, b), align_bytes=64)
+            rows = w1[512 * o : 512 * (o + 1), P * b : P * (b + 1)]
+            nc.sync.dma_start(out=wraw[o, b][:], in_=rows.rearrange("(p j) n -> p j n", j=4))
 
         nc.sync.dma_start(offs_t[:], offs)
         nc.sync.dma_start(ev_t[:], ev)
@@ -54,11 +58,13 @@ def tile_picked_ylift5_odd_p_kernel(tc, x_words, x_scales, w1, thr, offs, ev, od
                 in_=x_scales[:, 4 * q : 4 * q + 4, :].bitcast(I32),
             )
         load_words(0)
-        load_w(0)
-        load_words(1)
-        load_w(1)
         with nc.allow_non_contiguous_dma(reason="one threshold a partition"):
-            nc.gpsimd.dma_start(out=thr_t[:], in_=thr.rearrange("(b p) one -> p (b one)", p=P))
+            nc.sync.dma_start(out=thr_t[:], in_=thr.rearrange("(b p) one -> p (b one)", p=P))
+        load_w(0, 0)
+        load_words(1)
+        load_w(1, 0)
+        for o in range(PASSES):
+            load_w(o, 1)
 
         hi = keep.tile([P, BANDS], F32, name="hi")
         lo = keep.tile([P, BANDS], F32, name="lo")
@@ -66,14 +72,17 @@ def tile_picked_ylift5_odd_p_kernel(tc, x_words, x_scales, w1, thr, offs, ev, od
         gain = keep.tile([P, BANDS], F32, name="gain")
         nc.scalar.activation(hi[:], thr_t[:], ACT.Abs)
         nc.scalar.activation(lo[:], hi[:], ACT.Copy, scale=-1.0)
-        nc.scalar.activation(sg[:], thr_t[:], ACT.Sign)
-        nc.scalar.activation(gain[:], sg[:], ACT.Copy, scale=-0.125)
+        sg2 = keep.tile([P, BANDS], F32, name="sg2")
+        ungain = keep.tile([P, BANDS], F32, name="ungain")
+        nc.scalar.activation(sg[:], thr_t[:], ACT.Sign, scale=-1.0)
+        nc.scalar.activation(sg2[:], sg[:], ACT.Sign, bias=0.5)
+        nc.scalar.activation(gain[:], sg2[:], ACT.Copy, scale=0.125)
+        nc.scalar.activation(ungain[:], sg2[:], ACT.Copy, scale=8.0)
+        ident = keep.tile([P, P], F32, name="ident", align_bytes=64)
+        make_identity(nc, ident[:])
 
-        evn = [keep.tile([P, V + PAD], F32, name="evn%d" % b, align_bytes=64) for b in range(BANDS)]
-        odd = [keep.tile([P, V], F32, name="odd%d" % b, align_bytes=64) for b in range(BANDS)]
         clip = [keep.tile([P, V + 2 * PAD], F32, name="clip%d" % b, align_bytes=64) for b in range(BANDS)]
         for b in range(BANDS):
-            nc.gpsimd.memset(evn[b][:, V : V + PAD], 0.0)
             nc.gpsimd.memset(clip[b][:, 0:PAD], 0.0)
 
         wq = {}
@@ -81,10 +90,10 @@ def tile_picked_ylift5_odd_p_kernel(tc, x_words, x_scales, w1, thr, offs, ev, od
         wbf = {}
 
         def round_w(o, m0, m1):
-            wbf[o, m0] = keep.tile([P, (m1 - m0) * 4], BF16, name="wbf%d_%d" % (o, m0), align_bytes=64)
+            wbf[o, m0] = keep.tile([P, (m1 - m0) * 4], BF16, name="wbf", tag="wbf%d_%d" % (o, m0), align_bytes=64)
             nc.scalar.copy(
                 out=wbf[o, m0][:].rearrange("p (c i t) -> p c t i", i=4, t=4),
-                in_=wraw[o][:, :, m0:m1].rearrange("p t (c i) -> p c t i", i=4),
+                in_=wraw[o, m0 // P][:].rearrange("p t (c i) -> p c t i", i=4),
             )
 
         def quant_w(o, m0, m1):
@@ -97,25 +106,29 @@ def tile_picked_ylift5_odd_p_kernel(tc, x_words, x_scales, w1, thr, offs, ev, od
 
         gw = {}
 
-        def gather_words(o, a, b):
-            g = keep.tile([P, b - a], U32, name="gw%d_%d" % (o, a), align_bytes=64)
-            nc.vector.tensor_copy(g[:], xw[o][:].bitcast(U32).indirect(offs_t[:, a // 16 : b // 16]))
-            for lo_c, hi_c in PIECES:
-                if a <= lo_c and hi_c <= b:
-                    gw[o, lo_c] = g[:, lo_c - a : hi_c - a]
+        def gather_words(o, a, b, tag, cuts):
+            g = keep.tile([P, b - a], U32, name="gw", tag=tag, align_bytes=64)
+            for c0, c1 in cuts:
+                nc.vector.tensor_copy(
+                    g[:, c0 - a : c1 - a], xw[o][:].bitcast(U32).indirect(offs_t[:, c0 // 16 : c1 // 16])
+                )
+            for groups in GROUPS:
+                for c0, c1 in groups:
+                    if a <= c0 and c1 <= b:
+                        gw[o, c0, c1] = g[:, c0 - a : c1 - a]
 
         gs = keep.tile([P, S], U8, name="gs", align_bytes=64)
         acc = {}
         for b in range(BANDS):
-            for a, e in PIECES:
-                acc[b, a] = psum.tile([P, 512], F32, name="acc%d_%d" % (b, a))
+            for a, e in GROUPS[b]:
+                acc[b, a] = psum.tile([P, 512], F32, name="acc%d_%d" % (b, a), tag="bank%d" % len(acc))
 
         def mm(o, b, a, e):
             nc.tensor.matmul_mx(
                 out=acc[b, a][:, 0 : e - a],
                 lhsT=wq[o, b].bitcast(FP8X4),
                 lhsT_scale=ws[o, b],
-                rhs=gw[o, a].bitcast(FP8X4),
+                rhs=gw[o, a, e].bitcast(FP8X4),
                 rhs_scale=gs[4 * o : P, a:e],
                 start=(o == 0),
                 stop=(o == PASSES - 1),
@@ -124,50 +137,62 @@ def tile_picked_ylift5_odd_p_kernel(tc, x_words, x_scales, w1, thr, offs, ev, od
         y = [keep.tile([P, S], F32, name="y%d" % b, align_bytes=64) for b in range(BANDS)]
 
         nc.vector.tensor_copy(gs[:], xs[:].indirect(offs_t[:]))
-        gather_words(0, 0, S)
-        for o in range(PASSES):
-            for b in range(BANDS):
+        gather_words(0, 0, S, "gw0", ((0, S),))
+        for b in range(BANDS):
+            for o in range(PASSES):
                 round_w(o, P * b, P * (b + 1))
         quant_w(0, 0, P)
-        for a, e in PIECES:
+        for a, e in GROUPS[0]:
             mm(0, 0, a, e)
-        gather_words(1, 0, 512)
+        gather_words(1, 0, 512, "gw1", PIECES[:1])
         quant_w(1, 0, P)
-        gather_words(1, 512, 768)
-        gather_words(1, 768, 1024)
-        for a, e in PIECES:
+        gather_words(1, 512, S, "wbf1_0", PIECES[1:])
+        for a, e in GROUPS[0]:
             mm(1, 0, a, e)
-            nc.scalar.copy(out=y[0][:, a:e], in_=acc[0, a][:, 0 : e - a])
+            if e == S:
+                nc.vector.tensor_copy(y[0][:, a:e], acc[0, a][:, 0 : e - a])
+            else:
+                nc.scalar.copy(out=y[0][:, a:e], in_=acc[0, a][:, 0 : e - a])
         quant_w(0, P, N)
         quant_w(1, P, N)
         for o in range(PASSES):
-            for a, e in PIECES:
+            for a, e in GROUPS[1]:
                 mm(o, 1, a, e)
                 if o == PASSES - 1:
                     nc.scalar.copy(out=y[1][:, a:e], in_=acc[1, a][:, 0 : e - a])
 
-        pair = [keep.tile([P, V], F32, name="pair%d" % b, align_bytes=64) for b in range(BANDS)]
-        det = [keep.tile([P, V], F32, name="det%d" % b, align_bytes=64) for b in range(BANDS)]
+        pair = {}
+        det = {}
+        evn = {}
+        odd = {}
+
+        def lift_tiles(b):
+            evn[b] = keep.tile([P, V], F32, name="evn%d" % b, tag=("evn0", "pair0")[b], align_bytes=64)
+            odd[b] = keep.tile([P, V], F32, name="odd%d" % b, tag=("odd0", "det0")[b], align_bytes=64)
+            pair[b] = keep.tile([P, V], F32, name="pair%d" % b, tag="pair%d" % b, align_bytes=64)
+            det[b] = keep.tile([P, V], F32, name="det%d" % b, tag="det%d" % b, align_bytes=64)
+
         t1 = [keep.tile([P, V], F32, name="t1_%d" % b, align_bytes=64) for b in range(BANDS)]
         t2 = [keep.tile([P, V], F32, name="t2_%d" % b, align_bytes=64) for b in range(BANDS)]
         res = [keep.tile([P, V], F32, name="res%d" % b, align_bytes=64) for b in range(BANDS)]
 
-        def g_ev(b):
-            nc.vector.tensor_copy(evn[b][:, 0:V], y[b][:].indirect(ev_t[:]))
+        halves = ((0, V // 2), (V // 2, V))
 
-        def g_od(b):
-            nc.vector.tensor_copy(odd[b][:], y[b][:].indirect(od_t[:]))
-
-        def s_pair(b):
-            nc.vector.tensor_tensor(pair[b][:], evn[b][:, 0:V], evn[b][:, 1 : V + 1], ALU.add)
-
-        def s_det(b):
-            nc.vector.scalar_tensor_tensor(det[b][:], pair[b][:], -0.5, odd[b][:], ALU.mult, ALU.add)
-
-        def s_clip(b):
-            nc.vector.tensor_scalar(
-                clip[b][:, PAD : PAD + V], det[b][:], lo[:, b : b + 1], hi[:, b : b + 1], ALU.max, ALU.min
-            )
+        def predict(b):
+            lift_tiles(b)
+            nc.vector.tensor_copy(evn[b][:], y[b][:].indirect(ev_t[:]))
+            nc.scalar.copy(out=pair[b][:, V - 1 : V], in_=evn[b][:, V - 1 : V])
+            nc.vector.tensor_copy(odd[b][:, 0 : V // 2], y[b][:].indirect(od_t[:, 0 : V // 32]))
+            nc.vector.tensor_tensor(pair[b][:, 0 : V - 1], evn[b][:, 0 : V - 1], evn[b][:, 1:V], ALU.add)
+            nc.vector.tensor_copy(odd[b][:, V // 2 : V], y[b][:].indirect(od_t[:, V // 32 : V // 16]))
+            for a, e in halves:
+                nc.vector.scalar_tensor_tensor(
+                    det[b][:, a:e], pair[b][:, a:e], -0.5, odd[b][:, a:e], ALU.mult, ALU.add
+                )
+            for a, e in halves:
+                nc.vector.tensor_scalar(
+                    clip[b][:, PAD + a : PAD + e], det[b][:, a:e], lo[:, b : b + 1], hi[:, b : b + 1], ALU.max, ALU.min
+                )
             nc.scalar.activation(
                 clip[b][:, PAD + V : PAD + V + 1], clip[b][:, PAD + V - 1 : PAD + V], ACT.Copy, scale=-1.0
             )
@@ -186,20 +211,35 @@ def tile_picked_ylift5_odd_p_kernel(tc, x_words, x_scales, w1, thr, offs, ev, od
             )
             nc.sync.dma_start(out=out[P * b : P * (b + 1), a:e], in_=res[b][:, a:e])
 
-        g_ev(0)
-        g_od(0)
-        s_pair(0)
-        g_ev(1)
-        s_det(0)
-        g_od(1)
-        s_clip(0)
-        s_pair(1)
-        s_t1(0, 0, V)
-        s_det(1)
-        s_t2(0, 0, V)
-        s_clip(1)
-        s_out(0, 0, V)
-        halves = ((0, V // 2), (V // 2, V))
+        def filter_on_tensor(b):
+            blocks = range(V // P)
+            odd8 = keep.tile([P, V], F32, name="odd8", align_bytes=64)
+            clip6 = keep.tile([P, V], F32, name="clip6", align_bytes=64)
+            turned = keep.tile([P, V], F32, name="turned", align_bytes=64)
+            fwd = [psum.tile([P, 512], F32, name="fwd%d" % j, tag="bank%d" % ((6 + j) % 8)) for j in blocks]
+            back = psum.tile([P, V], F32, name="back", tag="bank2")
+            nc.scalar.activation(odd8[:], odd[b][:], ACT.Copy, scale=ungain[:, b : b + 1])
+            nc.scalar.activation(clip6[:], clip[b][:, PAD : PAD + V], ACT.Copy, scale=-6.0)
+            terms = ((odd8, 0), (clip[b], PAD - 1), (clip[b], PAD + 1), (clip6, 0))
+            for i, (src, shift) in enumerate(terms):
+                for j in blocks:
+                    nc.tensor.matmul(
+                        fwd[j][:, 0:P],
+                        src[:, shift + P * j : shift + P * (j + 1)],
+                        ident[:],
+                        start=(i == 0),
+                        stop=(i == len(terms) - 1),
+                        is_transpose=True,
+                    )
+            for j in blocks:
+                nc.scalar.copy(out=turned[:, P * j : P * (j + 1)], in_=fwd[j][:, 0:P])
+                nc.tensor.transpose(back[:, P * j : P * (j + 1)], turned[:, P * j : P * (j + 1)], ident[:])
+            nc.scalar.activation(res[b][:], back[:], ACT.Copy, scale=gain[:, b : b + 1])
+            nc.scalar.dma_start(out=out[P * b : P * (b + 1), :], in_=res[b][:])
+
+        predict(0)
+        filter_on_tensor(0)
+        predict(1)
         for step in (s_t1, s_t2, s_out):
             for a, e in halves:
                 step(1, a, e)

@@ -58,26 +58,14 @@ def tile_picked_ylift5_odd_p_kernel(tc, x_words, x_scales, w1, thr, offs, ev, od
                 in_=x_scales[:, 4 * q : 4 * q + 4, :].bitcast(I32),
             )
         load_words(0)
-        with nc.allow_non_contiguous_dma(reason="one threshold a partition"):
-            nc.sync.dma_start(out=thr_t[:], in_=thr.rearrange("(b p) one -> p (b one)", p=P))
         load_w(0, 0)
         load_words(1)
         load_w(1, 0)
         for o in range(PASSES):
             load_w(o, 1)
+        with nc.allow_non_contiguous_dma(reason="one threshold a partition"):
+            nc.sync.dma_start(out=thr_t[:], in_=thr.rearrange("(b p) one -> p (b one)", p=P))
 
-        hi = keep.tile([P, BANDS], F32, name="hi")
-        lo = keep.tile([P, BANDS], F32, name="lo")
-        sg = keep.tile([P, BANDS], F32, name="sg")
-        gain = keep.tile([P, BANDS], F32, name="gain")
-        nc.scalar.activation(hi[:], thr_t[:], ACT.Abs)
-        nc.scalar.activation(lo[:], hi[:], ACT.Copy, scale=-1.0)
-        sg2 = keep.tile([P, BANDS], F32, name="sg2")
-        ungain = keep.tile([P, BANDS], F32, name="ungain")
-        nc.scalar.activation(sg[:], thr_t[:], ACT.Sign, scale=-1.0)
-        nc.scalar.activation(sg2[:], sg[:], ACT.Sign, bias=0.5)
-        nc.scalar.activation(gain[:], sg2[:], ACT.Copy, scale=0.125)
-        nc.scalar.activation(ungain[:], sg2[:], ACT.Copy, scale=8.0)
         ident = keep.tile([P, P], F32, name="ident", align_bytes=64)
         make_identity(nc, ident[:])
 
@@ -134,7 +122,8 @@ def tile_picked_ylift5_odd_p_kernel(tc, x_words, x_scales, w1, thr, offs, ev, od
                 stop=(o == PASSES - 1),
             )
 
-        y = [keep.tile([P, S], F32, name="y%d" % b, align_bytes=64) for b in range(BANDS)]
+        y = [keep.tile([P, (T, S)[b]], F32, name="y%d" % b, align_bytes=64) for b in range(BANDS)]
+        nc.vector.memset(y[0][:, S:T], 0.0)
 
         nc.vector.tensor_copy(gs[:], xs[:].indirect(offs_t[:]))
         gather_words(0, 0, S, "gw0", ((0, S),))
@@ -161,41 +150,67 @@ def tile_picked_ylift5_odd_p_kernel(tc, x_words, x_scales, w1, thr, offs, ev, od
                 if o == PASSES - 1:
                     nc.scalar.copy(out=y[1][:, a:e], in_=acc[1, a][:, 0 : e - a])
 
+        hi = keep.tile([P, BANDS], F32, name="hi")
+        lo = keep.tile([P, BANDS], F32, name="lo")
+        sg = keep.tile([P, BANDS], F32, name="sg")
+        gain = keep.tile([P, BANDS], F32, name="gain")
+        nc.scalar.activation(hi[:], thr_t[:], ACT.Abs)
+        nc.scalar.activation(lo[:], hi[:], ACT.Copy, scale=-1.0)
+        sg2 = keep.tile([P, BANDS], F32, name="sg2")
+        ungain = keep.tile([P, BANDS], F32, name="ungain")
+        nc.scalar.activation(sg[:], thr_t[:], ACT.Sign, scale=-1.0)
+        nc.scalar.activation(sg2[:], sg[:], ACT.Sign, bias=0.5)
+        nc.scalar.activation(gain[:], sg2[:], ACT.Copy, scale=0.125)
+        nc.scalar.activation(ungain[:], sg2[:], ACT.Copy, scale=8.0)
+
         pair = {}
         det = {}
         evn = {}
         odd = {}
 
-        def lift_tiles(b):
-            evn[b] = keep.tile([P, V], F32, name="evn%d" % b, tag=("evn0", "pair0")[b], align_bytes=64)
-            odd[b] = keep.tile([P, V], F32, name="odd%d" % b, tag=("odd0", "det0")[b], align_bytes=64)
-            pair[b] = keep.tile([P, V], F32, name="pair%d" % b, tag="pair%d" % b, align_bytes=64)
-            det[b] = keep.tile([P, V], F32, name="det%d" % b, tag="det%d" % b, align_bytes=64)
-
+        for b in range(BANDS):
+            evn[b] = keep.tile([P, V], F32, name="evn%d" % b, align_bytes=64)
         t1 = [keep.tile([P, V], F32, name="t1_%d" % b, align_bytes=64) for b in range(BANDS)]
         t2 = [keep.tile([P, V], F32, name="t2_%d" % b, align_bytes=64) for b in range(BANDS)]
         res = [keep.tile([P, V], F32, name="res%d" % b, align_bytes=64) for b in range(BANDS)]
-
         halves = ((0, V // 2), (V // 2, V))
 
-        def predict(b):
-            lift_tiles(b)
-            nc.vector.tensor_copy(evn[b][:], y[b][:].indirect(ev_t[:]))
+        def pair_sums(b, tag):
+            pair[b] = keep.tile([P, V], F32, name="pair", tag=tag, align_bytes=64)
             nc.scalar.copy(out=pair[b][:, V - 1 : V], in_=evn[b][:, V - 1 : V])
-            nc.vector.tensor_copy(odd[b][:, 0 : V // 2], y[b][:].indirect(od_t[:, 0 : V // 32]))
-            nc.vector.tensor_tensor(pair[b][:, 0 : V - 1], evn[b][:, 0 : V - 1], evn[b][:, 1:V], ALU.add)
-            nc.vector.tensor_copy(odd[b][:, V // 2 : V], y[b][:].indirect(od_t[:, V // 32 : V // 16]))
-            for a, e in halves:
-                nc.vector.scalar_tensor_tensor(
-                    det[b][:, a:e], pair[b][:, a:e], -0.5, odd[b][:, a:e], ALU.mult, ALU.add
-                )
-            for a, e in halves:
+            nc.gpsimd.tensor_tensor(pair[b][:, 0 : V - 1], evn[b][:, 0 : V - 1], evn[b][:, 1:V], ALU.add)
+
+        def gather_odd(b, tag):
+            odd[b] = keep.tile([P, V], F32, name="odd", tag=tag, align_bytes=64)
+            nc.vector.tensor_copy(odd[b][:], y[b][:, 0:S].indirect(od_t[:]))
+
+        def clamp(b, cuts):
+            for a, e in cuts:
                 nc.vector.tensor_scalar(
                     clip[b][:, PAD + a : PAD + e], det[b][:, a:e], lo[:, b : b + 1], hi[:, b : b + 1], ALU.max, ALU.min
                 )
             nc.scalar.activation(
                 clip[b][:, PAD + V : PAD + V + 1], clip[b][:, PAD + V - 1 : PAD + V], ACT.Copy, scale=-1.0
             )
+
+        def predict0():
+            nc.vector.tensor_scalar(evn[0][:], y[0][:].indirect(ev_t[:]), -0.5, 0.0, ALU.mult, ALU.add)
+            gather_odd(0, "odd0")
+            pair_sums(0, "pair0")
+            det[0] = keep.tile([P, V], F32, name="det", tag="det0", align_bytes=64)
+            nc.gpsimd.tensor_tensor(det[0][:], pair[0][:], odd[0][:], ALU.add)
+            nc.vector.tensor_copy(evn[1][:], y[1][:].indirect(ev_t[:]))
+            clamp(0, ((0, V),))
+
+        def predict1():
+            gather_odd(1, "pair0")
+            pair_sums(1, "det0")
+            det[1] = keep.tile([P, V], F32, name="det", tag="det1", align_bytes=64)
+            for a, e in halves:
+                nc.vector.scalar_tensor_tensor(
+                    det[1][:, a:e], pair[1][:, a:e], -0.5, odd[1][:, a:e], ALU.mult, ALU.add
+                )
+            clamp(1, halves)
 
         def s_t1(b, a, e):
             nc.vector.scalar_tensor_tensor(
@@ -217,7 +232,7 @@ def tile_picked_ylift5_odd_p_kernel(tc, x_words, x_scales, w1, thr, offs, ev, od
             clip6 = keep.tile([P, V], F32, name="clip6", align_bytes=64)
             turned = keep.tile([P, V], F32, name="turned", align_bytes=64)
             fwd = [psum.tile([P, 512], F32, name="fwd%d" % j, tag="bank%d" % ((6 + j) % 8)) for j in blocks]
-            back = psum.tile([P, V], F32, name="back", tag="bank2")
+            back = [psum.tile([P, 512], F32, name="back%d" % h, tag="bank%d" % (2 + h)) for h in range(2)]
             nc.scalar.activation(odd8[:], odd[b][:], ACT.Copy, scale=ungain[:, b : b + 1])
             nc.scalar.activation(clip6[:], clip[b][:, PAD : PAD + V], ACT.Copy, scale=-6.0)
             terms = ((odd8, 0), (clip[b], PAD - 1), (clip[b], PAD + 1), (clip6, 0))
@@ -233,13 +248,15 @@ def tile_picked_ylift5_odd_p_kernel(tc, x_words, x_scales, w1, thr, offs, ev, od
                     )
             for j in blocks:
                 nc.scalar.copy(out=turned[:, P * j : P * (j + 1)], in_=fwd[j][:, 0:P])
-                nc.tensor.transpose(back[:, P * j : P * (j + 1)], turned[:, P * j : P * (j + 1)], ident[:])
-            nc.scalar.activation(res[b][:], back[:], ACT.Copy, scale=gain[:, b : b + 1])
-            nc.scalar.dma_start(out=out[P * b : P * (b + 1), :], in_=res[b][:])
+                col = P * (j % 2)
+                nc.tensor.transpose(back[j // 2][:, col : col + P], turned[:, P * j : P * (j + 1)], ident[:])
+            for h, (a, e) in enumerate(halves):
+                nc.scalar.activation(res[b][:, a:e], back[h][:, 0 : e - a], ACT.Copy, scale=gain[:, b : b + 1])
+                nc.scalar.dma_start(out=out[P * b : P * (b + 1), a:e], in_=res[b][:, a:e])
 
-        predict(0)
+        predict0()
         filter_on_tensor(0)
-        predict(1)
+        predict1()
         for step in (s_t1, s_t2, s_out):
             for a, e in halves:
                 step(1, a, e)

from contextlib import ExitStack

import concourse.mybir as mybir
from concourse.masks import make_identity

K, T, S, N, V = 1024, 2048, 1024, 256, 512
FLOPS = 2 * K * S * N

F32 = mybir.dt.float32
BF16 = mybir.dt.bfloat16
I32 = mybir.dt.int32
U32 = mybir.dt.uint32
U16 = mybir.dt.uint16
U8 = mybir.dt.uint8
FP8X4 = mybir.dt.float8_e4m3fn_x4
ALU = mybir.AluOpType
ACT = mybir.ActivationFunctionType

P = 128
PASSES = 2
BANDS = N // P
PIECES = ((0, 512), (512, 768), (768, 1024))
GROUPS = (((0, 512), (512, 768), (768, 896), (896, 1024)), ((0, 512), (512, 1024)))
PAD = 8


def tile_picked_ylift5_odd_p_kernel(tc, x_words, x_scales, w1, thr, offs, ev, od, out):
    nc = tc.nc
    with ExitStack() as ctx:
        keep = ctx.enter_context(tc.tile_pool(name="keep", bufs=1))
        psum = ctx.enter_context(tc.psum_pool(name="psum", bufs=1))

        offs_t = keep.tile([P, S // 16], U16, name="offs_t")
        ev_t = keep.tile([P, V // 16], U16, name="ev_t")
        od_t = keep.tile([P, V // 16], U16, name="od_t")
        xw = [keep.tile([P, T], I32, name="xw%d" % o, align_bytes=64) for o in range(PASSES)]
        xs = keep.tile([P, T], U8, name="xs", align_bytes=64)
        wraw = {}
        thr_t = keep.tile([P, BANDS], F32, name="thr_t")

        nc.gpsimd.memset(xs[:, 0 : T // 2].bitcast(I32), 0)
        nc.vector.memset(xs[:, T // 2 : T].bitcast(I32), 0)

        def load_words(o):
            nc.sync.dma_start(out=xw[o][:], in_=x_words[o].rearrange("p n t -> p (n t)").bitcast(I32))

        def load_w(o, b):
            wraw[o, b] = keep.tile([P, 4, P], F32, name="wraw%d_%d" % (o, b), align_bytes=64)
            rows = w1[512 * o : 512 * (o + 1), P * b : P * (b + 1)]
            nc.sync.dma_start(out=wraw[o, b][:], in_=rows.rearrange("(p j) n -> p j n", j=4))

        nc.sync.dma_start(offs_t[:], offs)
        nc.sync.dma_start(ev_t[:], ev)
        nc.sync.dma_start(od_t[:], od)
        for q in range(4):
            nc.sync.dma_start(
                out=xs[32 * q : 32 * q + 8, :].bitcast(I32),
                in_=x_scales[:, 4 * q : 4 * q + 4, :].bitcast(I32),
            )
        load_words(0)
        load_w(0, 0)
        load_words(1)
        load_w(1, 0)
        for o in range(PASSES):
            load_w(o, 1)
        with nc.allow_non_contiguous_dma(reason="one threshold a partition"):
            nc.sync.dma_start(out=thr_t[:], in_=thr.rearrange("(b p) one -> p (b one)", p=P))

        ident = keep.tile([P, P], F32, name="ident", align_bytes=64)
        make_identity(nc, ident[:])

        clip = [keep.tile([P, V + 2 * PAD], F32, name="clip%d" % b, align_bytes=64) for b in range(BANDS)]
        for b in range(BANDS):
            nc.gpsimd.memset(clip[b][:, 0:PAD], 0.0)

        wq = {}
        ws = {}
        wbf = {}

        def round_w(o, m0, m1):
            wbf[o, m0] = keep.tile([P, (m1 - m0) * 4], BF16, name="wbf", tag="wbf%d_%d" % (o, m0), align_bytes=64)
            nc.scalar.copy(
                out=wbf[o, m0][:].rearrange("p (c i t) -> p c t i", i=4, t=4),
                in_=wraw[o, m0 // P][:].rearrange("p t (c i) -> p c t i", i=4),
            )

        def quant_w(o, m0, m1):
            codes = keep.tile([P, m1 - m0], U32, name="wq%d_%d" % (o, m0), align_bytes=64)
            scales = keep.tile([P, m1 - m0], U8, name="ws%d_%d" % (o, m0), align_bytes=64)
            nc.vector.quantize_mx(out=codes[:].bitcast(FP8X4), scales=scales[:], in_=wbf[o, m0][:])
            for m in range(m0, m1, P):
                wq[o, m // P] = codes[:, m - m0 : m - m0 + P]
                ws[o, m // P] = scales[:, m - m0 : m - m0 + P]

        gw = {}

        def gather_words(o, a, b, tag, cuts):
            g = keep.tile([P, b - a], U32, name="gw", tag=tag, align_bytes=64)
            for c0, c1 in cuts:
                nc.vector.tensor_copy(
                    g[:, c0 - a : c1 - a], xw[o][:].bitcast(U32).indirect(offs_t[:, c0 // 16 : c1 // 16])
                )
            for groups in GROUPS:
                for c0, c1 in groups:
                    if a <= c0 and c1 <= b:
                        gw[o, c0, c1] = g[:, c0 - a : c1 - a]

        gs = keep.tile([P, S], U8, name="gs", align_bytes=64)
        acc = {}
        for b in range(BANDS):
            for a, e in GROUPS[b]:
                acc[b, a] = psum.tile([P, 512], F32, name="acc%d_%d" % (b, a), tag="bank%d" % len(acc))

        def mm(o, b, a, e):
            nc.tensor.matmul_mx(
                out=acc[b, a][:, 0 : e - a],
                lhsT=wq[o, b].bitcast(FP8X4),
                lhsT_scale=ws[o, b],
                rhs=gw[o, a, e].bitcast(FP8X4),
                rhs_scale=gs[4 * o : P, a:e],
                start=(o == 0),
                stop=(o == PASSES - 1),
            )

        y = [keep.tile([P, (T, S)[b]], F32, name="y%d" % b, align_bytes=64) for b in range(BANDS)]
        nc.vector.memset(y[0][:, S:T], 0.0)

        nc.vector.tensor_copy(gs[:], xs[:].indirect(offs_t[:]))
        gather_words(0, 0, S, "gw0", ((0, S),))
        for b in range(BANDS):
            for o in range(PASSES):
                round_w(o, P * b, P * (b + 1))
        quant_w(0, 0, P)
        for a, e in GROUPS[0]:
            mm(0, 0, a, e)
        gather_words(1, 0, 512, "gw1", PIECES[:1])
        quant_w(1, 0, P)
        gather_words(1, 512, S, "wbf1_0", PIECES[1:])
        for a, e in GROUPS[0]:
            mm(1, 0, a, e)
            if e == S:
                nc.vector.tensor_copy(y[0][:, a:e], acc[0, a][:, 0 : e - a])
            else:
                nc.scalar.copy(out=y[0][:, a:e], in_=acc[0, a][:, 0 : e - a])
        quant_w(0, P, N)
        quant_w(1, P, N)
        for o in range(PASSES):
            for a, e in GROUPS[1]:
                mm(o, 1, a, e)
                if o == PASSES - 1:
                    nc.scalar.copy(out=y[1][:, a:e], in_=acc[1, a][:, 0 : e - a])

        hi = keep.tile([P, BANDS], F32, name="hi")
        lo = keep.tile([P, BANDS], F32, name="lo")
        sg = keep.tile([P, BANDS], F32, name="sg")
        gain = keep.tile([P, BANDS], F32, name="gain")
        nc.scalar.activation(hi[:], thr_t[:], ACT.Abs)
        nc.scalar.activation(lo[:], hi[:], ACT.Copy, scale=-1.0)
        sg2 = keep.tile([P, BANDS], F32, name="sg2")
        ungain = keep.tile([P, BANDS], F32, name="ungain")
        nc.scalar.activation(sg[:], thr_t[:], ACT.Sign, scale=-1.0)
        nc.scalar.activation(sg2[:], sg[:], ACT.Sign, bias=0.5)
        nc.scalar.activation(gain[:], sg2[:], ACT.Copy, scale=0.125)
        nc.scalar.activation(ungain[:], sg2[:], ACT.Copy, scale=8.0)

        pair = {}
        det = {}
        evn = {}
        odd = {}

        for b in range(BANDS):
            evn[b] = keep.tile([P, V], F32, name="evn%d" % b, align_bytes=64)
        t1 = [keep.tile([P, V], F32, name="t1_%d" % b, align_bytes=64) for b in range(BANDS)]
        t2 = [keep.tile([P, V], F32, name="t2_%d" % b, align_bytes=64) for b in range(BANDS)]
        res = [keep.tile([P, V], F32, name="res%d" % b, align_bytes=64) for b in range(BANDS)]
        halves = ((0, V // 2), (V // 2, V))

        def pair_sums(b, tag):
            pair[b] = keep.tile([P, V], F32, name="pair", tag=tag, align_bytes=64)
            nc.scalar.copy(out=pair[b][:, V - 1 : V], in_=evn[b][:, V - 1 : V])
            nc.gpsimd.tensor_tensor(pair[b][:, 0 : V - 1], evn[b][:, 0 : V - 1], evn[b][:, 1:V], ALU.add)

        def gather_odd(b, tag):
            odd[b] = keep.tile([P, V], F32, name="odd", tag=tag, align_bytes=64)
            nc.vector.tensor_copy(odd[b][:], y[b][:, 0:S].indirect(od_t[:]))

        def clamp(b, cuts):
            for a, e in cuts:
                nc.vector.tensor_scalar(
                    clip[b][:, PAD + a : PAD + e], det[b][:, a:e], lo[:, b : b + 1], hi[:, b : b + 1], ALU.max, ALU.min
                )
            nc.scalar.activation(
                clip[b][:, PAD + V : PAD + V + 1], clip[b][:, PAD + V - 1 : PAD + V], ACT.Copy, scale=-1.0
            )

        def predict0():
            nc.vector.tensor_scalar(evn[0][:], y[0][:].indirect(ev_t[:]), -0.5, 0.0, ALU.mult, ALU.add)
            gather_odd(0, "odd0")
            pair_sums(0, "pair0")
            det[0] = keep.tile([P, V], F32, name="det", tag="det0", align_bytes=64)
            nc.gpsimd.tensor_tensor(det[0][:], pair[0][:], odd[0][:], ALU.add)
            nc.vector.tensor_copy(evn[1][:], y[1][:].indirect(ev_t[:]))
            clamp(0, ((0, V),))

        def predict1():
            gather_odd(1, "pair0")
            pair_sums(1, "det0")
            det[1] = keep.tile([P, V], F32, name="det", tag="det1", align_bytes=64)
            for a, e in halves:
                nc.vector.scalar_tensor_tensor(
                    det[1][:, a:e], pair[1][:, a:e], -0.5, odd[1][:, a:e], ALU.mult, ALU.add
                )
            clamp(1, halves)

        def s_t1(b, a, e):
            nc.vector.scalar_tensor_tensor(
                t1[b][:, a:e], clip[b][:, PAD + a : PAD + e], -6.0, clip[b][:, PAD + a - 1 : PAD + e - 1], ALU.mult, ALU.add
            )

        def s_t2(b, a, e):
            nc.vector.tensor_tensor(t2[b][:, a:e], t1[b][:, a:e], clip[b][:, PAD + a + 1 : PAD + e + 1], ALU.add)

        def s_out(b, a, e):
            nc.vector.scalar_tensor_tensor(
                res[b][:, a:e], t2[b][:, a:e], gain[:, b : b + 1], odd[b][:, a:e], ALU.mult, ALU.add
            )
            nc.sync.dma_start(out=out[P * b : P * (b + 1), a:e], in_=res[b][:, a:e])

        def filter_on_tensor(b):
            blocks = range(V // P)
            odd8 = keep.tile([P, V], F32, name="odd8", align_bytes=64)
            clip6 = keep.tile([P, V], F32, name="clip6", align_bytes=64)
            turned = keep.tile([P, V], F32, name="turned", align_bytes=64)
            fwd = [psum.tile([P, 512], F32, name="fwd%d" % j, tag="bank%d" % ((6 + j) % 8)) for j in blocks]
            back = [psum.tile([P, 512], F32, name="back%d" % h, tag="bank%d" % (2 + h)) for h in range(2)]
            nc.scalar.activation(odd8[:], odd[b][:], ACT.Copy, scale=ungain[:, b : b + 1])
            nc.scalar.activation(clip6[:], clip[b][:, PAD : PAD + V], ACT.Copy, scale=-6.0)
            terms = ((odd8, 0), (clip[b], PAD - 1), (clip[b], PAD + 1), (clip6, 0))
            for i, (src, shift) in enumerate(terms):
                for j in blocks:
                    nc.tensor.matmul(
                        fwd[j][:, 0:P],
                        src[:, shift + P * j : shift + P * (j + 1)],
                        ident[:],
                        start=(i == 0),
                        stop=(i == len(terms) - 1),
                        is_transpose=True,
                    )
            for j in blocks:
                nc.scalar.copy(out=turned[:, P * j : P * (j + 1)], in_=fwd[j][:, 0:P])
                col = P * (j % 2)
                nc.tensor.transpose(back[j // 2][:, col : col + P], turned[:, P * j : P * (j + 1)], ident[:])
            for h, (a, e) in enumerate(halves):
                nc.scalar.activation(res[b][:, a:e], back[h][:, 0 : e - a], ACT.Copy, scale=gain[:, b : b + 1])
                nc.scalar.dma_start(out=out[P * b : P * (b + 1), a:e], in_=res[b][:, a:e])

        predict0()
        filter_on_tensor(0)
        predict1()
        for step in (s_t1, s_t2, s_out):
            for a, e in halves:
                step(1, a, e)
